import numpy as np
import ml_dtypes


def mxq(x, axis, fmt="e4m3"):
    dtype, down = {"e4m3": (ml_dtypes.float8_e4m3fn, 7), "e5m2": (ml_dtypes.float8_e5m2, 14)}[fmt]
    v = np.moveaxis(np.asarray(x, np.float32).astype(ml_dtypes.bfloat16).astype(np.float64), axis, -1)
    blocks = v.reshape(v.shape[:-1] + (-1, 32))
    amax = np.abs(blocks).max(-1, keepdims=True)
    byte = np.maximum(np.where(amax > 0, np.frexp(amax)[1] - 1 + 127, 0) - down, 1)
    scale = np.exp2(byte - 127.0)
    codes = (blocks / scale).astype(np.float32).astype(dtype).astype(np.float64)
    return np.moveaxis((codes * scale).reshape(v.shape), -1, axis)


WIDE = False


def mx_kscale(k, group=512):
    if not WIDE:
        return np.ones(k)
    levels = np.array([10, -10, 5, -5, 0])
    if group != 512:
        return np.exp2(np.random.permutation(np.resize(levels, k // group))).repeat(group)
    if k % 512:
        return np.exp2(np.random.permutation(np.resize(levels, k // 32))).repeat(32)
    a = np.empty((k // 512, 16))
    for p in range(k // 512):
        a[p, :8] = np.random.permutation(np.resize(levels, 8))
        for g in range(8):
            far = levels[np.abs(levels - a[p, g]) >= 10]
            a[p, g + 8] = far[np.random.randint(len(far))]
    return np.exp2(a.ravel()).repeat(32)


def f64(x):
    return np.asarray(x).astype(np.float64)


G, D, M, N = 4, 256, 128, 1024


def setup_inputs():
    n = np.random.standard_normal
    s = mx_kscale(D, 0)[:, None]
    return {
        "x": (n((G, D, N)) * s).astype(np.float32),
        "w": (n((G, D, M)) / np.sqrt(D) / s).astype(np.float32),
        "u": (n((G, D, M)) / np.sqrt(D) / s).astype(np.float32),
        "b": (0.5 * n((G, M, 1))).astype(np.float32),
        "r": n((G, M, N)).astype(np.float32),
    }


def reference(x, w, u, b, r):
    xq = mxq(f64(x), 1, "e4m3")
    h = mxq(f64(w), 1, "e4m3").transpose(0, 2, 1) @ xq
    g = mxq(f64(u), 1, "e4m3").transpose(0, 2, 1) @ xq
    h = h + f64(b)
    y = np.tanh(h) * g
    y = y + f64(r)
    return y

@@ -1,0 +1,134 @@
+from contextlib import ExitStack
+
+import concourse.mybir as mybir
+
+G, D, M, N = 4, 256, 128, 1024
+FLOPS = 2 * 2 * G * D * M * N
+
+F32 = mybir.dt.float32
+BF16 = mybir.dt.bfloat16
+U32 = mybir.dt.uint32
+U8 = mybir.dt.uint8
+FP8X4 = mybir.dt.float8_e4m3fn_x4
+TANH = mybir.ActivationFunctionType.Tanh
+MULT = mybir.AluOpType.mult
+ADD = mybir.AluOpType.add
+
+P = 128
+PACK = 4
+ROWS = 64
+W = 512
+
+LOADS = [["x",0,0,256],["w",0,0],["x",0,256,512],["w",0,1],["x",1,0,512],["w",1,0],["w",1,1],["x",2,0,512],["r",0],["x",3,0,512],["r",1],["r",2],["r",3]]
+ORDER = [["I",0,0,128,"V"],["I",0,128,256,"S"],["Iw",0,0,"V"],["B"],["Qw",0,0,1],["I",0,256,416,"V"],["I",0,416,512,"S"],["Iw",0,1,"S"],["Q",0,0,512],["P",0,0,0],["P",0,0,1],["Qw",0,1,2],["P",0,1,0],["P",0,1,1],["T",0,0],["I",1,0,384,"V"],["I",1,384,512,"S"],["T",0,1],["M",0,0],["Q",1,0,512],["P",1,0,0],["P",1,0,1],["P",1,1,0],["P",1,1,1],["Iw",1,0,"S"],["M",0,1],["Iw",1,1,"V"],["T",1,0],["T",1,1],["Qw",1,0,2],["M",1,0],["I",2,0,160,"V"],["I",2,160,512,"S"],["M",1,1],["A",0,0,1,"V"],["Q",2,0,512],["P",2,0,0],["P",2,0,1],["P",2,1,0],["P",2,1,1],["A",0,1,2,"V"],["T",2,0],["I",3,0,256,"V"],["I",3,256,512,"S"],["T",2,1],["M",2,0],["Q",3,0,512],["P",3,0,0],["P",3,0,1],["P",3,1,0],["P",3,1,1],["A",1,0,2,"V"],["T",3,0],["T",3,1],["M",2,1],["A",2,0,1,"V"],["M",3,0],["A",2,1,2,"V"],["M",3,1],["A",3,0,1,"V"],["A",3,1,2,"V"]]
+STORES = [[0,0,2],[1,0,2],[2,0,2],[3,0,1],[3,1,2]]
+
+
+def tile_rows_gglu_tanh_bias_res_kernel(tc, x, w, u, b, r, out):
+    nc = tc.nc
+    with ExitStack() as ctx:
+        sb = ctx.enter_context(tc.tile_pool(name="sb", bufs=1))
+        ps = ctx.enter_context(tc.psum_pool(name="ps", bufs=1))
+        ctx.enter_context(tc.manual_schedule())
+
+        def tiles(prefix, count, shape, dtype):
+            return [sb.tile(shape, dtype, name="%s%d" % (prefix, i), align_bytes=64) for i in range(count)]
+
+        x_raw = tiles("x_raw", 4, [P, PACK, W], F32)
+        x_bf = tiles("x_bf", 4, [P, W, PACK], BF16)
+        x_codes = tiles("x_codes", 4, [P, W], U32)
+        x_scales = tiles("x_scales", 4, [P, W], U8)
+        wt_raw = tiles("wt_raw", 4, [P, PACK, M], F32)
+        wt_bf = tiles("wt_bf", 2, [P, 2, M, PACK], BF16)
+        wt_codes = tiles("wt_codes", 2, [P, 2, M], U32)
+        wt_scales = tiles("wt_scales", 2, [P, 2, M], U8)
+        r_sb = tiles("r_sb", 4, [P, 2, W], F32)
+        act = tiles("act", 4, [P, 2, W], F32)
+        gated = tiles("gated", 4, [P, 2, W], F32)
+        y = tiles("y", 4, [P, 2, W], F32)
+        b_rows = sb.tile([P, 32], F32, align_bytes=64)
+        b_cols = sb.tile([P, 32], F32, align_bytes=64)
+        banks = [[[ps.tile([M, W], F32, name="ps%d%d%d" % (k, c, s)) for s in range(2)] for c in range(2)] for k in range(2)]
+
+        x_pairs = x.rearrange("(q c) (p j) n -> q (c p) j n", c=2, j=PACK)
+        wt_pairs = [t.rearrange("(q c) (p j) m -> q (c p) j m", c=2, j=PACK) for t in (w, u)]
+        r_pairs = r.rearrange("(q c) m n -> q m c n", c=2)
+        out_pairs = out.rearrange("(q c) m n -> q m c n", c=2)
+
+        nc.vector.memset(b_rows[:], 0.0)
+        for quad in range(4):
+            nc.scalar.dma_start(out=b_rows[32 * quad : 32 * quad + G, :], in_=b[:, 32 * quad : 32 * quad + 32, 0])
+
+        for ld in LOADS:
+            if ld[0] == "x":
+                t, c0, c1 = ld[1], ld[2], ld[3]
+                base = (t % 2) * W
+                nc.sync.dma_start(out=x_raw[t][:, :, c0:c1], in_=x_pairs[t // 2][:, :, base + c0 : base + c1])
+            elif ld[0] == "w":
+                q, k = ld[1], ld[2]
+                nc.sync.dma_start(out=wt_raw[2 * q + k][:], in_=wt_pairs[k][q])
+            else:
+                t = ld[1]
+                base = (t % 2) * W
+                nc.sync.dma_start(out=r_sb[t][:], in_=r_pairs[t // 2][:, :, base : base + W])
+
+        def interleave(eng, dst, src):
+            dst = dst.rearrange("p (c i) j -> p c j i", i=4)
+            src = src.rearrange("p j (c i) -> p c j i", i=4)
+            if eng == "V":
+                nc.vector.tensor_copy(out=dst, in_=src)
+            else:
+                nc.scalar.copy(out=dst, in_=src)
+
+        for op in ORDER:
+            kind = op[0]
+            if kind == "B":
+                nc.vector.transpose(out=b_cols[:], in_=b_rows[:])
+            elif kind == "I":
+                t, c0, c1, eng = op[1], op[2], op[3], op[4]
+                interleave(eng, x_bf[t][:, c0:c1, :], x_raw[t][:, :, c0:c1])
+            elif kind == "Iw":
+                q, k, eng = op[1], op[2], op[3]
+                interleave(eng, wt_bf[q][:, k], wt_raw[2 * q + k][:])
+            elif kind == "Q":
+                t, c0, c1 = op[1], op[2], op[3]
+                nc.vector.quantize_mx(
+                    out=x_codes[t][:, c0:c1].bitcast(FP8X4),
+                    scales=x_scales[t][:, c0:c1],
+                    in_=x_bf[t][:, c0:c1, :].rearrange("p n j -> p (n j)"),
+                )
+            elif kind == "Qw":
+                q, k0, k1 = op[1], op[2], op[3]
+                nc.vector.quantize_mx(
+                    out=wt_codes[q][:, k0:k1].rearrange("p k m -> p (k m)").bitcast(FP8X4),
+                    scales=wt_scales[q][:, k0:k1].rearrange("p k m -> p (k m)"),
+                    in_=wt_bf[q][:, k0:k1].rearrange("p k m j -> p (k m j)"),
+                )
+            elif kind == "P":
+                t, k, c = op[1], op[2], op[3]
+                rows = slice(ROWS * c, ROWS * (c + 1))
+                nc.tensor.matmul_mx(
+                    out=banks[k][c][t % 2][:],
+                    lhsT=wt_codes[t // 2][rows, k].bitcast(FP8X4),
+                    lhsT_scale=wt_scales[t // 2][rows, k],
+                    rhs=x_codes[t][rows, :].bitcast(FP8X4),
+                    rhs_scale=x_scales[t][rows, :],
+                    start=True,
+                    stop=True,
+                )
+            elif kind == "T":
+                t, c = op[1], op[2]
+                g = 2 * (t // 2) + c
+                nc.scalar.activation(out=act[t][:, c], in_=banks[0][c][t % 2][:], func=TANH, bias=b_cols[:, g : g + 1])
+            elif kind == "M":
+                t, c = op[1], op[2]
+                nc.vector.tensor_tensor(out=gated[t][:, c], in0=act[t][:, c], in1=banks[1][c][t % 2][:], op=MULT)
+            elif kind == "A":
+                t, c0, c1, eng = op[1], op[2], op[3], op[4]
+                e = nc.vector if eng == "V" else nc.gpsimd
+                e.tensor_tensor(out=y[t][:, c0:c1], in0=gated[t][:, c0:c1], in1=r_sb[t][:, c0:c1], op=ADD)
+
+        for st in STORES:
+            t, c0, c1 = st[0], st[1], st[2]
+            base = (t % 2) * W
+            nc.sync.dma_start(out=out_pairs[t // 2][:, c0:c1, base : base + W], in_=y[t][:, c0:c1])

@@ -17,11 +17,15 @@ ADD = mybir.AluOpType.add
 P = 128
 PACK = 4
 ROWS = 64
-W = 512
+NM = 128
 
-LOADS = [["x",0,0,256],["w",0,0],["x",0,256,512],["w",0,1],["x",1,0,512],["w",1,0],["w",1,1],["x",2,0,512],["r",0],["x",3,0,512],["r",1],["r",2],["r",3]]
-ORDER = [["I",0,0,128,"V"],["I",0,128,256,"S"],["Iw",0,0,"V"],["B"],["Qw",0,0,1],["I",0,256,416,"V"],["I",0,416,512,"S"],["Iw",0,1,"S"],["Q",0,0,512],["P",0,0,0],["P",0,0,1],["Qw",0,1,2],["P",0,1,0],["P",0,1,1],["T",0,0],["I",1,0,384,"V"],["I",1,384,512,"S"],["T",0,1],["M",0,0],["Q",1,0,512],["P",1,0,0],["P",1,0,1],["P",1,1,0],["P",1,1,1],["Iw",1,0,"S"],["M",0,1],["Iw",1,1,"V"],["T",1,0],["T",1,1],["Qw",1,0,2],["M",1,0],["I",2,0,160,"V"],["I",2,160,512,"S"],["M",1,1],["A",0,0,1,"V"],["Q",2,0,512],["P",2,0,0],["P",2,0,1],["P",2,1,0],["P",2,1,1],["A",0,1,2,"V"],["T",2,0],["I",3,0,256,"V"],["I",3,256,512,"S"],["T",2,1],["M",2,0],["Q",3,0,512],["P",3,0,0],["P",3,0,1],["P",3,1,0],["P",3,1,1],["A",1,0,2,"V"],["T",3,0],["T",3,1],["M",2,1],["A",2,0,1,"V"],["M",3,0],["A",2,1,2,"V"],["M",3,1],["A",3,0,1,"V"],["A",3,1,2,"V"]]
-STORES = [[0,0,2],[1,0,2],[2,0,2],[3,0,1],[3,1,2]]
+PIECES = [[0,0,256],[0,256,512],[0,512,768],[0,768,1024],[1,0,256],[1,256,512],[1,512,768],[1,768,1024]]
+UNITS = [[0],[1],[2],[3],[4],[5],[6],[7]]
+SPLIT = [224,192,192,160,160,256,0,0]
+LOADS = [[["u",0]],[["x",0]],[["w",0]],[["x",1]],[["x",2]],[["x",3]],[["w",1]],[["x",4]],[["u",1]],[["x",5]],[["x",6]],[["r",0],["r",1]],[["x",7]],[["r",2],["r",3]],[["r",4],["r",5]],[["r",6],["r",7]]]
+ORDER = [["J",0,1,"V"],["W",0,1,"V"],["I",0,"V"],["I",0,"S"],["J",0,0,"V"],["Q",0],["W",0,0,"V"],["h",0,0],["B"],["I",1,"V"],["I",1,"S"],["g",0,0],["h",0,1],["T",0,0],["Q",1],["g",0,1],["I",2,"V"],["I",2,"S"],["h",1,0],["T",0,1],["M",0,0],["g",1,0],["Q",2],["h",1,1],["T",1,0],["g",1,1],["M",0,1],["I",3,"S"],["I",3,"V"],["h",2,0],["T",1,1],["g",2,0],["J",1,0,"V"],["h",2,1],["T",2,0],["Q",3],["g",2,1],["M",1,0],["M",1,1],["h",3,0],["I",4,"S"],["I",4,"V"],["g",3,0],["h",3,1],["T",2,1],["W",1,0,"V"],["g",3,1],["T",3,0],["Q",4],["J",1,1,"S"],["M",2,0],["M",2,1],["h",4,0],["M",3,0],["W",1,1,"V"],["T",4,0],["I",5,"V"],["T",3,1],["g",4,0],["h",4,1],["I",6,"S"],["Q",5],["g",4,1],["M",3,1],["M",4,0],["h",5,0],["g",5,0],["A",[0,1],0,2,"V"],["h",5,1],["T",5,0],["g",5,1],["T",4,1],["T",5,1],["Q",6],["I",7,"S"],["M",5,1],["M",5,0],["h",6,0],["M",4,1],["g",6,0],["h",6,1],["A",[2,3],0,2,"V"],["T",6,0],["g",6,1],["T",6,1],["Q",7],["A",[4,5],0,2,"V"],["h",7,0],["g",7,0],["h",7,1],["T",7,0],["M",6,1],["g",7,1],["M",6,0],["T",7,1],["M",7,0],["A",[6],0,2,"V"],["M",7,1],["A",[7],0,1,"V"],["A",[7],1,2,"V"]]
+STORES = [[[0,1],0,2],[[2,3],0,2],[[4,5],0,2],[[6],0,2],[[7],0,1],[[7],1,2]]
+YGROUPS = [[0,1],[2,3],[4,5],[6],[7]]
 
 
 def tile_rows_gglu_tanh_bias_res_kernel(tc, x, w, u, b, r, out):
@@ -31,46 +35,62 @@ def tile_rows_gglu_tanh_bias_res_kernel(tc, x, w, u, b, r, out):
         ps = ctx.enter_context(tc.psum_pool(name="ps", bufs=1))
         ctx.enter_context(tc.manual_schedule())
 
-        def tiles(prefix, count, shape, dtype):
-            return [sb.tile(shape, dtype, name="%s%d" % (prefix, i), align_bytes=64) for i in range(count)]
+        def tile(name, shape, dtype):
+            return sb.tile(shape, dtype, name=name, align_bytes=64)
 
-        x_raw = tiles("x_raw", 4, [P, PACK, W], F32)
-        x_bf = tiles("x_bf", 4, [P, W, PACK], BF16)
-        x_codes = tiles("x_codes", 4, [P, W], U32)
-        x_scales = tiles("x_scales", 4, [P, W], U8)
-        wt_raw = tiles("wt_raw", 4, [P, PACK, M], F32)
-        wt_bf = tiles("wt_bf", 2, [P, 2, M, PACK], BF16)
-        wt_codes = tiles("wt_codes", 2, [P, 2, M], U32)
-        wt_scales = tiles("wt_scales", 2, [P, 2, M], U8)
-        r_sb = tiles("r_sb", 4, [P, 2, W], F32)
-        act = tiles("act", 4, [P, 2, W], F32)
-        gated = tiles("gated", 4, [P, 2, W], F32)
-        y = tiles("y", 4, [P, 2, W], F32)
-        b_rows = sb.tile([P, 32], F32, align_bytes=64)
-        b_cols = sb.tile([P, 32], F32, align_bytes=64)
-        banks = [[[ps.tile([M, W], F32, name="ps%d%d%d" % (k, c, s)) for s in range(2)] for c in range(2)] for k in range(2)]
+        span = [(PIECES[ps_[0]][0], PIECES[ps_[0]][1], PIECES[ps_[-1]][2]) for ps_ in UNITS]
+        unit_of = {i: t for t, ps_ in enumerate(UNITS) for i in ps_}
+        x_bf = [tile("x_bf%d" % i, [P, p[2] - p[1], PACK], BF16) for i, p in enumerate(PIECES)]
+        x_codes = [tile("x_codes%d" % t, [P, s[2] - s[1]], U32) for t, s in enumerate(span)]
+        x_scales = [tile("x_scales%d" % t, [P, s[2] - s[1]], U8) for t, s in enumerate(span)]
+        wt_bf = [[tile("wt_bf%d%d" % (q, k), [P, M, PACK], BF16) for k in range(2)] for q in range(2)]
+        wt_codes = [[tile("wt_codes%d%d" % (q, k), [P, M], U32) for k in range(2)] for q in range(2)]
+        wt_scales = [[tile("wt_scales%d%d" % (q, k), [P, M], U8) for k in range(2)] for q in range(2)]
+        act = [tile("act%d" % t, [P, 2, s[2] - s[1]], F32) for t, s in enumerate(span)]
+        gated, y = {}, {}
+        for us in YGROUPS:
+            c0, c1 = span[us[0]][1], span[us[-1]][2]
+            gt = tile("gated%d" % us[0], [P, 2, c1 - c0], F32)
+            yt = tile("y%d" % us[0], [P, 2, c1 - c0], F32)
+            for t in us:
+                gated[t] = (gt, c0)
+                y[t] = (yt, c0)
+        b_rows = sb.tile([P, 32 * G], F32, align_bytes=64)
+        b_cols = sb.tile([P, 32 * G], F32, align_bytes=64)
+        banks = [[[ps.tile([M, 512], F32, name="ps%d%d%d" % (k, c, s)) for s in range(2)] for c in range(2)] for k in range(2)]
 
         x_pairs = x.rearrange("(q c) (p j) n -> q (c p) j n", c=2, j=PACK)
-        wt_pairs = [t.rearrange("(q c) (p j) m -> q (c p) j m", c=2, j=PACK) for t in (w, u)]
+        wt_pairs = [t.rearrange("(q c) (p j) m -> (c p) q j m", c=2, j=PACK) for t in (w, u)]
         r_pairs = r.rearrange("(q c) m n -> q m c n", c=2)
         out_pairs = out.rearrange("(q c) m n -> q m c n", c=2)
 
-        nc.vector.memset(b_rows[:], 0.0)
-        for quad in range(4):
-            nc.scalar.dma_start(out=b_rows[32 * quad : 32 * quad + G, :], in_=b[:, 32 * quad : 32 * quad + 32, 0])
+        nc.gpsimd.memset(b_rows[:], 0.0)
+        nc.scalar.dma_start(
+            out=b_rows[0:P:32, :].rearrange("q (g j) -> q g j", g=G),
+            in_=b.rearrange("g (q j) o -> q g (j o)", j=32),
+        )
 
+        x_raw, wt_raw, r_sb = {}, {}, {}
         for ld in LOADS:
-            if ld[0] == "x":
-                t, c0, c1 = ld[1], ld[2], ld[3]
-                base = (t % 2) * W
-                nc.sync.dma_start(out=x_raw[t][:, :, c0:c1], in_=x_pairs[t // 2][:, :, base + c0 : base + c1])
-            elif ld[0] == "w":
-                q, k = ld[1], ld[2]
-                nc.sync.dma_start(out=wt_raw[2 * q + k][:], in_=wt_pairs[k][q])
+            kind, first, last = ld[0][0], ld[0][1], ld[-1][1]
+            if kind == "x":
+                q, c0, c1 = PIECES[first][0], PIECES[first][1], PIECES[last][2]
+                t_ = tile("x_raw%d" % first, [P, PACK, c1 - c0], F32)
+                nc.sync.dma_start(out=t_[:], in_=x_pairs[q][:, :, c0:c1])
+                for e in ld:
+                    x_raw[e[1]] = (t_, c0)
+            elif kind == "r":
+                q, c0, c1 = span[first][0], span[first][1], span[last][2]
+                t_ = tile("r_sb%d" % first, [P, 2, c1 - c0], F32)
+                nc.sync.dma_start(out=t_[:], in_=r_pairs[q][:, :, c0:c1])
+                for e in ld:
+                    r_sb[e[1]] = (t_, c0)
             else:
-                t = ld[1]
-                base = (t % 2) * W
-                nc.sync.dma_start(out=r_sb[t][:], in_=r_pairs[t // 2][:, :, base : base + W])
+                k = 0 if kind == "w" else 1
+                t_ = tile("wt_raw%d%d" % (first, k), [P, last + 1 - first, PACK, M], F32)
+                nc.sync.dma_start(out=t_[:], in_=wt_pairs[k][:, first : last + 1])
+                for e in ld:
+                    wt_raw[(e[1], k)] = t_[:, e[1] - first]
 
         def interleave(eng, dst, src):
             dst = dst.rearrange("p (c i) j -> p c j i", i=4)
@@ -80,55 +100,75 @@ def tile_rows_gglu_tanh_bias_res_kernel(tc, x, w, u, b, r, out):
             else:
                 nc.scalar.copy(out=dst, in_=src)
 
+        def cols(entry, c0, c1):
+            return slice(c0 - entry[1], c1 - entry[1])
+
         for op in ORDER:
             kind = op[0]
             if kind == "B":
                 nc.vector.transpose(out=b_cols[:], in_=b_rows[:])
             elif kind == "I":
-                t, c0, c1, eng = op[1], op[2], op[3], op[4]
-                interleave(eng, x_bf[t][:, c0:c1, :], x_raw[t][:, :, c0:c1])
-            elif kind == "Iw":
+                i, eng = op[1], op[2]
+                width = PIECES[i][2] - PIECES[i][1]
+                a0, a1 = (0, SPLIT[i]) if eng == "V" else (SPLIT[i], width)
+                base = PIECES[i][1] - x_raw[i][1]
+                interleave(eng, x_bf[i][:, a0:a1, :], x_raw[i][0][:, :, base + a0 : base + a1])
+            elif kind == "J":
                 q, k, eng = op[1], op[2], op[3]
-                interleave(eng, wt_bf[q][:, k], wt_raw[2 * q + k][:])
+                interleave(eng, wt_bf[q][k][:], wt_raw[(q, k)])
             elif kind == "Q":
-                t, c0, c1 = op[1], op[2], op[3]
+                i = op[1]
+                t = unit_of[i]
+                sl = slice(PIECES[i][1] - span[t][1], PIECES[i][2] - span[t][1])
                 nc.vector.quantize_mx(
-                    out=x_codes[t][:, c0:c1].bitcast(FP8X4),
-                    scales=x_scales[t][:, c0:c1],
-                    in_=x_bf[t][:, c0:c1, :].rearrange("p n j -> p (n j)"),
+                    out=x_codes[t][:, sl].bitcast(FP8X4),
+                    scales=x_scales[t][:, sl],
+                    in_=x_bf[i][:].rearrange("p n j -> p (n j)"),
                 )
-            elif kind == "Qw":
-                q, k0, k1 = op[1], op[2], op[3]
+            elif kind == "W":
+                q, k = op[1], op[2]
                 nc.vector.quantize_mx(
-                    out=wt_codes[q][:, k0:k1].rearrange("p k m -> p (k m)").bitcast(FP8X4),
-                    scales=wt_scales[q][:, k0:k1].rearrange("p k m -> p (k m)"),
-                    in_=wt_bf[q][:, k0:k1].rearrange("p k m j -> p (k m j)"),
+                    out=wt_codes[q][k][:].bitcast(FP8X4),
+                    scales=wt_scales[q][k][:],
+                    in_=wt_bf[q][k][:].rearrange("p m j -> p (m j)"),
                 )
-            elif kind == "P":
-                t, k, c = op[1], op[2], op[3]
+            elif kind == "h" or kind == "g":
+                t, c, k = op[1], op[2], (0 if kind == "h" else 1)
                 rows = slice(ROWS * c, ROWS * (c + 1))
-                nc.tensor.matmul_mx(
-                    out=banks[k][c][t % 2][:],
-                    lhsT=wt_codes[t // 2][rows, k].bitcast(FP8X4),
-                    lhsT_scale=wt_scales[t // 2][rows, k],
-                    rhs=x_codes[t][rows, :].bitcast(FP8X4),
-                    rhs_scale=x_scales[t][rows, :],
-                    start=True,
-                    stop=True,
-                )
+                q = span[t][0]
+                for n0 in range(0, span[t][2] - span[t][1], NM):
+                    nc.tensor.matmul_mx(
+                        out=banks[k][c][t % 2][:, n0 : n0 + NM],
+                        lhsT=wt_codes[q][k][rows, :].bitcast(FP8X4),
+                        lhsT_scale=wt_scales[q][k][rows, :],
+                        rhs=x_codes[t][rows, n0 : n0 + NM].bitcast(FP8X4),
+                        rhs_scale=x_scales[t][rows, n0 : n0 + NM],
+                        start=True,
+                        stop=True,
+                    )
             elif kind == "T":
                 t, c = op[1], op[2]
-                g = 2 * (t // 2) + c
-                nc.scalar.activation(out=act[t][:, c], in_=banks[0][c][t % 2][:], func=TANH, bias=b_cols[:, g : g + 1])
+                g = 2 * span[t][0] + c
+                width = span[t][2] - span[t][1]
+                nc.scalar.activation(out=act[t][:, c], in_=banks[0][c][t % 2][:, :width], func=TANH, bias=b_cols[:, 32 * g : 32 * g + 1])
             elif kind == "M":
                 t, c = op[1], op[2]
-                nc.vector.tensor_tensor(out=gated[t][:, c], in0=act[t][:, c], in1=banks[1][c][t % 2][:], op=MULT)
-            elif kind == "A":
-                t, c0, c1, eng = op[1], op[2], op[3], op[4]
-                e = nc.vector if eng == "V" else nc.gpsimd
-                e.tensor_tensor(out=y[t][:, c0:c1], in0=gated[t][:, c0:c1], in1=r_sb[t][:, c0:c1], op=ADD)
+                width = span[t][2] - span[t][1]
+                sl = cols(gated[t], span[t][1], span[t][2])
+                nc.vector.tensor_tensor(out=gated[t][0][:, c, sl], in0=act[t][:, c], in1=banks[1][c][t % 2][:, :width], op=MULT)
+            else:
+                us, c0, c1 = op[1], op[2], op[3]
+                n0, n1 = span[us[0]][1], span[us[-1]][2]
+                t = us[0]
+                e = nc.vector if op[4] == "V" else nc.gpsimd
+                e.tensor_tensor(
+                    out=y[t][0][:, c0:c1, cols(y[t], n0, n1)],
+                    in0=gated[t][0][:, c0:c1, cols(gated[t], n0, n1)],
+                    in1=r_sb[t][0][:, c0:c1, cols(r_sb[t], n0, n1)],
+                    op=ADD,
+                )
 
-        for st in STORES:
-            t, c0, c1 = st[0], st[1], st[2]
-            base = (t % 2) * W
-            nc.sync.dma_start(out=out_pairs[t // 2][:, c0:c1, base : base + W], in_=y[t][:, c0:c1])
+        for us, c0, c1 in STORES:
+            q, n0, n1 = span[us[0]][0], span[us[0]][1], span[us[-1]][2]
+            t = us[0]
+            nc.sync.dma_start(out=out_pairs[q][:, c0:c1, n0:n1], in_=y[t][0][:, c0:c1, cols(y[t], n0, n1)])

@@ -21,11 +21,11 @@ NM = 128
 
 PIECES = [[0,0,256],[0,256,512],[0,512,768],[0,768,1024],[1,0,256],[1,256,512],[1,512,768],[1,768,1024]]
 UNITS = [[0],[1],[2],[3],[4],[5],[6],[7]]
-SPLIT = [224,192,192,160,160,256,0,0]
-LOADS = [[["u",0]],[["x",0]],[["w",0]],[["x",1]],[["x",2]],[["x",3]],[["w",1]],[["x",4]],[["u",1]],[["x",5]],[["x",6]],[["r",0],["r",1]],[["x",7]],[["r",2],["r",3]],[["r",4],["r",5]],[["r",6],["r",7]]]
-ORDER = [["J",0,1,"V"],["W",0,1,"V"],["I",0,"V"],["I",0,"S"],["J",0,0,"V"],["Q",0],["W",0,0,"V"],["h",0,0],["B"],["I",1,"V"],["I",1,"S"],["g",0,0],["h",0,1],["T",0,0],["Q",1],["g",0,1],["I",2,"V"],["I",2,"S"],["h",1,0],["T",0,1],["M",0,0],["g",1,0],["Q",2],["h",1,1],["T",1,0],["g",1,1],["M",0,1],["I",3,"S"],["I",3,"V"],["h",2,0],["T",1,1],["g",2,0],["J",1,0,"V"],["h",2,1],["T",2,0],["Q",3],["g",2,1],["M",1,0],["M",1,1],["h",3,0],["I",4,"S"],["I",4,"V"],["g",3,0],["h",3,1],["T",2,1],["W",1,0,"V"],["g",3,1],["T",3,0],["Q",4],["J",1,1,"S"],["M",2,0],["M",2,1],["h",4,0],["M",3,0],["W",1,1,"V"],["T",4,0],["I",5,"V"],["T",3,1],["g",4,0],["h",4,1],["I",6,"S"],["Q",5],["g",4,1],["M",3,1],["M",4,0],["h",5,0],["g",5,0],["A",[0,1],0,2,"V"],["h",5,1],["T",5,0],["g",5,1],["T",4,1],["T",5,1],["Q",6],["I",7,"S"],["M",5,1],["M",5,0],["h",6,0],["M",4,1],["g",6,0],["h",6,1],["A",[2,3],0,2,"V"],["T",6,0],["g",6,1],["T",6,1],["Q",7],["A",[4,5],0,2,"V"],["h",7,0],["g",7,0],["h",7,1],["T",7,0],["M",6,1],["g",7,1],["M",6,0],["T",7,1],["M",7,0],["A",[6],0,2,"V"],["M",7,1],["A",[7],0,1,"V"],["A",[7],1,2,"V"]]
-STORES = [[[0,1],0,2],[[2,3],0,2],[[4,5],0,2],[[6],0,2],[[7],0,1],[[7],1,2]]
-YGROUPS = [[0,1],[2,3],[4,5],[6],[7]]
+SPLIT = [256,0,0,160,0,192,0,0]
+LOADS = [[["x",0],["x",1],["x",2],["x",3]],[["w",0]],[["u",0]],[["w",1]],[["x",4],["x",5],["x",6]],[["r",0,1],["r",1,1],["r",2,1],["r",3,1]],[["u",1]],[["r",0,0],["r",1,0],["r",2,0],["r",3,0]],[["x",7]],[["r",4,0],["r",5,0],["r",6,0],["r",7,0]],[["r",4,1],["r",5,1],["r",6,1],["r",7,1]]]
+ORDER = [["B"],["I",0,"V"],["I",1,"S"],["J",0,0,"V"],["Q",0],["I",2,"S"],["W",0,0,"V"],["J",0,1,"V"],["h",0,0],["h",0,1],["Q",1],["W",0,1,"V"],["J",1,0,"V"],["T",0,0],["g",0,0],["g",0,1],["I",3,"V"],["T",0,1],["h",1,0],["h",1,1],["I",3,"S"],["Q",2],["g",1,0],["g",1,1],["M",0,0],["T",1,0],["M",0,1],["h",2,0],["h",2,1],["T",1,1],["Q",3],["g",2,0],["M",1,0],["g",2,1],["T",2,0],["M",1,1],["h",3,0],["h",3,1],["T",2,1],["g",3,0],["M",2,0],["g",3,1],["T",3,1],["M",2,1],["T",3,0],["W",1,0,"V"],["I",5,"V"],["I",5,"S"],["I",4,"S"],["M",3,1],["M",3,0],["A",[0,1,2,3],1,2,"V"],["J",1,1,"S"],["Q",4],["I",6,"S"],["W",1,1,"V"],["Q",5],["h",4,0],["h",4,1],["A",[0,1,2,3],0,1,"V"],["g",4,0],["g",4,1],["h",5,0],["h",5,1],["T",4,1],["g",5,0],["g",5,1],["T",4,0],["T",5,0],["Q",6],["T",5,1],["M",4,0],["I",7,"S"],["M",4,1],["h",6,0],["h",6,1],["M",5,0],["g",6,0],["M",5,1],["g",6,1],["A",[4,5],0,1,"V"],["T",6,0],["T",6,1],["Q",7],["M",6,0],["M",6,1],["h",7,0],["h",7,1],["A",[6],0,1,"V"],["g",7,0],["g",7,1],["A",[4,5],1,2,"V"],["T",7,0],["T",7,1],["A",[6],1,2,"V"],["M",7,0],["M",7,1],["A",[7],0,1,"V"],["A",[7],1,2,"V"]]
+STORES = [[[0,1,2,3],0,1],[[0,1,2,3],1,2],[[4,5,6],0,1],[[4,5,6],1,2],[[7],0,1],[[7],1,2]]
+YGROUPS = [[0,1,2,3],[4,5,6],[7]]
 
 
 def tile_rows_gglu_tanh_bias_res_kernel(tc, x, w, u, b, r, out):
@@ -81,10 +81,11 @@ def tile_rows_gglu_tanh_bias_res_kernel(tc, x, w, u, b, r, out):
                     x_raw[e[1]] = (t_, c0)
             elif kind == "r":
                 q, c0, c1 = span[first][0], span[first][1], span[last][2]
-                t_ = tile("r_sb%d" % first, [P, 2, c1 - c0], F32)
-                nc.sync.dma_start(out=t_[:], in_=r_pairs[q][:, :, c0:c1])
+                k0, k1 = ld[0][2], ld[-1][2] + 1
+                t_ = tile("r_sb%d%d" % (first, k0), [P, k1 - k0, c1 - c0], F32)
+                nc.sync.dma_start(out=t_[:], in_=r_pairs[q][:, k0:k1, c0:c1])
                 for e in ld:
-                    r_sb[e[1]] = (t_, c0)
+                    r_sb[(e[1], e[2])] = (t_, c0, k0)
             else:
                 k = 0 if kind == "w" else 1
                 t_ = tile("wt_raw%d%d" % (first, k), [P, last + 1 - first, PACK, M], F32)
@@ -160,11 +161,12 @@ def tile_rows_gglu_tanh_bias_res_kernel(tc, x, w, u, b, r, out):
                 us, c0, c1 = op[1], op[2], op[3]
                 n0, n1 = span[us[0]][1], span[us[-1]][2]
                 t = us[0]
+                rt = r_sb[(t, c0)]
                 e = nc.vector if op[4] == "V" else nc.gpsimd
                 e.tensor_tensor(
                     out=y[t][0][:, c0:c1, cols(y[t], n0, n1)],
                     in0=gated[t][0][:, c0:c1, cols(gated[t], n0, n1)],
-                    in1=r_sb[t][0][:, c0:c1, cols(r_sb[t], n0, n1)],
+                    in1=rt[0][:, c0 - rt[2] : c1 - rt[2], cols(rt, n0, n1)],
                     op=ADD,
                 )
 

from contextlib import ExitStack

import concourse.mybir as mybir

G, D, M, N = 4, 256, 128, 1024
FLOPS = 2 * 2 * G * D * M * N

F32 = mybir.dt.float32
BF16 = mybir.dt.bfloat16
U32 = mybir.dt.uint32
U8 = mybir.dt.uint8
FP8X4 = mybir.dt.float8_e4m3fn_x4
TANH = mybir.ActivationFunctionType.Tanh
MULT = mybir.AluOpType.mult
ADD = mybir.AluOpType.add

P = 128
PACK = 4
ROWS = 64
NM = 128

PIECES = [[0,0,256],[0,256,512],[0,512,768],[0,768,1024],[1,0,256],[1,256,512],[1,512,768],[1,768,1024]]
UNITS = [[0],[1],[2],[3],[4],[5],[6],[7]]
SPLIT = [256,0,0,160,0,192,0,0]
LOADS = [[["x",0],["x",1],["x",2],["x",3]],[["w",0]],[["u",0]],[["w",1]],[["x",4],["x",5],["x",6]],[["r",0,1],["r",1,1],["r",2,1],["r",3,1]],[["u",1]],[["r",0,0],["r",1,0],["r",2,0],["r",3,0]],[["x",7]],[["r",4,0],["r",5,0],["r",6,0],["r",7,0]],[["r",4,1],["r",5,1],["r",6,1],["r",7,1]]]
ORDER = [["B"],["I",0,"V"],["I",1,"S"],["J",0,0,"V"],["Q",0],["I",2,"S"],["W",0,0,"V"],["J",0,1,"V"],["h",0,0],["h",0,1],["Q",1],["W",0,1,"V"],["J",1,0,"V"],["T",0,0],["g",0,0],["g",0,1],["I",3,"V"],["T",0,1],["h",1,0],["h",1,1],["I",3,"S"],["Q",2],["g",1,0],["g",1,1],["M",0,0],["T",1,0],["M",0,1],["h",2,0],["h",2,1],["T",1,1],["Q",3],["g",2,0],["M",1,0],["g",2,1],["T",2,0],["M",1,1],["h",3,0],["h",3,1],["T",2,1],["g",3,0],["M",2,0],["g",3,1],["T",3,1],["M",2,1],["T",3,0],["W",1,0,"V"],["I",5,"V"],["I",5,"S"],["I",4,"S"],["M",3,1],["M",3,0],["A",[0,1,2,3],1,2,"V"],["J",1,1,"S"],["Q",4],["I",6,"S"],["W",1,1,"V"],["Q",5],["h",4,0],["h",4,1],["A",[0,1,2,3],0,1,"V"],["g",4,0],["g",4,1],["h",5,0],["h",5,1],["T",4,1],["g",5,0],["g",5,1],["T",4,0],["T",5,0],["Q",6],["T",5,1],["M",4,0],["I",7,"S"],["M",4,1],["h",6,0],["h",6,1],["M",5,0],["g",6,0],["M",5,1],["g",6,1],["A",[4,5],0,1,"V"],["T",6,0],["T",6,1],["Q",7],["M",6,0],["M",6,1],["h",7,0],["h",7,1],["A",[6],0,1,"V"],["g",7,0],["g",7,1],["A",[4,5],1,2,"V"],["T",7,0],["T",7,1],["A",[6],1,2,"V"],["M",7,0],["M",7,1],["A",[7],0,1,"V"],["A",[7],1,2,"V"]]
STORES = [[[0,1,2,3],0,1],[[0,1,2,3],1,2],[[4,5,6],0,1],[[4,5,6],1,2],[[7],0,1],[[7],1,2]]
YGROUPS = [[0,1,2,3],[4,5,6],[7]]


def tile_rows_gglu_tanh_bias_res_kernel(tc, x, w, u, b, r, out):
    nc = tc.nc
    with ExitStack() as ctx:
        sb = ctx.enter_context(tc.tile_pool(name="sb", bufs=1))
        ps = ctx.enter_context(tc.psum_pool(name="ps", bufs=1))
        ctx.enter_context(tc.manual_schedule())

        def tile(name, shape, dtype):
            return sb.tile(shape, dtype, name=name, align_bytes=64)

        span = [(PIECES[ps_[0]][0], PIECES[ps_[0]][1], PIECES[ps_[-1]][2]) for ps_ in UNITS]
        unit_of = {i: t for t, ps_ in enumerate(UNITS) for i in ps_}
        x_bf = [tile("x_bf%d" % i, [P, p[2] - p[1], PACK], BF16) for i, p in enumerate(PIECES)]
        x_codes = [tile("x_codes%d" % t, [P, s[2] - s[1]], U32) for t, s in enumerate(span)]
        x_scales = [tile("x_scales%d" % t, [P, s[2] - s[1]], U8) for t, s in enumerate(span)]
        wt_bf = [[tile("wt_bf%d%d" % (q, k), [P, M, PACK], BF16) for k in range(2)] for q in range(2)]
        wt_codes = [[tile("wt_codes%d%d" % (q, k), [P, M], U32) for k in range(2)] for q in range(2)]
        wt_scales = [[tile("wt_scales%d%d" % (q, k), [P, M], U8) for k in range(2)] for q in range(2)]
        act = [tile("act%d" % t, [P, 2, s[2] - s[1]], F32) for t, s in enumerate(span)]
        gated, y = {}, {}
        for us in YGROUPS:
            c0, c1 = span[us[0]][1], span[us[-1]][2]
            gt = tile("gated%d" % us[0], [P, 2, c1 - c0], F32)
            yt = tile("y%d" % us[0], [P, 2, c1 - c0], F32)
            for t in us:
                gated[t] = (gt, c0)
                y[t] = (yt, c0)
        b_rows = sb.tile([P, 32 * G], F32, align_bytes=64)
        b_cols = sb.tile([P, 32 * G], F32, align_bytes=64)
        banks = [[[ps.tile([M, 512], F32, name="ps%d%d%d" % (k, c, s)) for s in range(2)] for c in range(2)] for k in range(2)]

        x_pairs = x.rearrange("(q c) (p j) n -> q (c p) j n", c=2, j=PACK)
        wt_pairs = [t.rearrange("(q c) (p j) m -> (c p) q j m", c=2, j=PACK) for t in (w, u)]
        r_pairs = r.rearrange("(q c) m n -> q m c n", c=2)
        out_pairs = out.rearrange("(q c) m n -> q m c n", c=2)

        nc.gpsimd.memset(b_rows[:], 0.0)
        nc.scalar.dma_start(
            out=b_rows[0:P:32, :].rearrange("q (g j) -> q g j", g=G),
            in_=b.rearrange("g (q j) o -> q g (j o)", j=32),
        )

        x_raw, wt_raw, r_sb = {}, {}, {}
        for ld in LOADS:
            kind, first, last = ld[0][0], ld[0][1], ld[-1][1]
            if kind == "x":
                q, c0, c1 = PIECES[first][0], PIECES[first][1], PIECES[last][2]
                t_ = tile("x_raw%d" % first, [P, PACK, c1 - c0], F32)
                nc.sync.dma_start(out=t_[:], in_=x_pairs[q][:, :, c0:c1])
                for e in ld:
                    x_raw[e[1]] = (t_, c0)
            elif kind == "r":
                q, c0, c1 = span[first][0], span[first][1], span[last][2]
                k0, k1 = ld[0][2], ld[-1][2] + 1
                t_ = tile("r_sb%d%d" % (first, k0), [P, k1 - k0, c1 - c0], F32)
                nc.sync.dma_start(out=t_[:], in_=r_pairs[q][:, k0:k1, c0:c1])
                for e in ld:
                    r_sb[(e[1], e[2])] = (t_, c0, k0)
            else:
                k = 0 if kind == "w" else 1
                t_ = tile("wt_raw%d%d" % (first, k), [P, last + 1 - first, PACK, M], F32)
                nc.sync.dma_start(out=t_[:], in_=wt_pairs[k][:, first : last + 1])
                for e in ld:
                    wt_raw[(e[1], k)] = t_[:, e[1] - first]

        def interleave(eng, dst, src):
            dst = dst.rearrange("p (c i) j -> p c j i", i=4)
            src = src.rearrange("p j (c i) -> p c j i", i=4)
            if eng == "V":
                nc.vector.tensor_copy(out=dst, in_=src)
            else:
                nc.scalar.copy(out=dst, in_=src)

        def cols(entry, c0, c1):
            return slice(c0 - entry[1], c1 - entry[1])

        for op in ORDER:
            kind = op[0]
            if kind == "B":
                nc.vector.transpose(out=b_cols[:], in_=b_rows[:])
            elif kind == "I":
                i, eng = op[1], op[2]
                width = PIECES[i][2] - PIECES[i][1]
                a0, a1 = (0, SPLIT[i]) if eng == "V" else (SPLIT[i], width)
                base = PIECES[i][1] - x_raw[i][1]
                interleave(eng, x_bf[i][:, a0:a1, :], x_raw[i][0][:, :, base + a0 : base + a1])
            elif kind == "J":
                q, k, eng = op[1], op[2], op[3]
                interleave(eng, wt_bf[q][k][:], wt_raw[(q, k)])
            elif kind == "Q":
                i = op[1]
                t = unit_of[i]
                sl = slice(PIECES[i][1] - span[t][1], PIECES[i][2] - span[t][1])
                nc.vector.quantize_mx(
                    out=x_codes[t][:, sl].bitcast(FP8X4),
                    scales=x_scales[t][:, sl],
                    in_=x_bf[i][:].rearrange("p n j -> p (n j)"),
                )
            elif kind == "W":
                q, k = op[1], op[2]
                nc.vector.quantize_mx(
                    out=wt_codes[q][k][:].bitcast(FP8X4),
                    scales=wt_scales[q][k][:],
                    in_=wt_bf[q][k][:].rearrange("p m j -> p (m j)"),
                )
            elif kind == "h" or kind == "g":
                t, c, k = op[1], op[2], (0 if kind == "h" else 1)
                rows = slice(ROWS * c, ROWS * (c + 1))
                q = span[t][0]
                for n0 in range(0, span[t][2] - span[t][1], NM):
                    nc.tensor.matmul_mx(
                        out=banks[k][c][t % 2][:, n0 : n0 + NM],
                        lhsT=wt_codes[q][k][rows, :].bitcast(FP8X4),
                        lhsT_scale=wt_scales[q][k][rows, :],
                        rhs=x_codes[t][rows, n0 : n0 + NM].bitcast(FP8X4),
                        rhs_scale=x_scales[t][rows, n0 : n0 + NM],
                        start=True,
                        stop=True,
                    )
            elif kind == "T":
                t, c = op[1], op[2]
                g = 2 * span[t][0] + c
                width = span[t][2] - span[t][1]
                nc.scalar.activation(out=act[t][:, c], in_=banks[0][c][t % 2][:, :width], func=TANH, bias=b_cols[:, 32 * g : 32 * g + 1])
            elif kind == "M":
                t, c = op[1], op[2]
                width = span[t][2] - span[t][1]
                sl = cols(gated[t], span[t][1], span[t][2])
                nc.vector.tensor_tensor(out=gated[t][0][:, c, sl], in0=act[t][:, c], in1=banks[1][c][t % 2][:, :width], op=MULT)
            else:
                us, c0, c1 = op[1], op[2], op[3]
                n0, n1 = span[us[0]][1], span[us[-1]][2]
                t = us[0]
                rt = r_sb[(t, c0)]
                e = nc.vector if op[4] == "V" else nc.gpsimd
                e.tensor_tensor(
                    out=y[t][0][:, c0:c1, cols(y[t], n0, n1)],
                    in0=gated[t][0][:, c0:c1, cols(gated[t], n0, n1)],
                    in1=rt[0][:, c0 - rt[2] : c1 - rt[2], cols(rt, n0, n1)],
                    op=ADD,
                )

        for us, c0, c1 in STORES:
            q, n0, n1 = span[us[0]][0], span[us[0]][1], span[us[-1]][2]
            t = us[0]
            nc.sync.dma_start(out=out_pairs[q][:, c0:c1, n0:n1], in_=y[t][0][:, c0:c1, cols(y[t], n0, n1)])
